import numpy as np, ml_dtypes
CORES = [66,70,74,78,82,86,90,94,98,102,106,110,114,118,122,126]
N = 16
import mx_ref
NC, KT = 256, 1
OWNER = [2,2,2,5,5,2,5,2,2,2,5,2,5,2,5,2]
BF = ml_dtypes.bfloat16
def setup_inputs(rng):
    def f(*shape):
        return mx_ref.flush((rng.standard_normal(shape, dtype=np.float32) * np.exp2(rng.integers(-2, 3, shape[:-1] + (1,)))).astype(BF))
    return {"w": f(N, 128, KT * 512), "x": f(N, 128, KT * 4 * NC)}
def setup_inputs_blocks(rng):
    d = setup_inputs(rng)
    for k in ("w", "x"): d[k] = mx_ref.spread(d[k], rng, 4)
    return d
def setup_inputs_wide(rng):
    d = setup_inputs(rng)
    for k in ("w", "x"): d[k] = mx_ref.flush((d[k].astype(np.float32) * np.exp2(rng.integers(-8, 9, (N, 1, 1))).astype(np.float32)).astype(BF))
    return d
def setup_inputs_zeros(rng):
    d = setup_inputs(rng); v = d["x"].reshape(N, 128, -1, 4).copy()
    v[np.broadcast_to((rng.random((N, 1, v.shape[2], 1)) < 0.33), v.shape)] = 0
    d["x"] = v.reshape(d["x"].shape)
    return d
def reference(w, x):
    y = np.zeros((N, 128, NC), np.float32)
    for r in range(N):
        for t in range(KT):
            p = mx_ref.matmul(mx_ref.quantize(w[OWNER[r]][:, 512 * t:512 * t + 512]), mx_ref.quantize(x[r][:, 4 * NC * t:4 * NC * t + 4 * NC]))
            y[r] = p if t == 0 else y[r] + p
    return {"y": y}

from concourse.bass import DstId, RemoteDMATransfer
from concourse.mybir import dt

SCRATCH = {
    "wt": ("sbuf", [128, 512], "bfloat16"),
    "xt": ("sbuf", [128, 1024], "bfloat16"),
    "wq_own": ("sbuf", [128, 128], "float8_e4m3fn_x4"),
    "ws_own": ("sbuf", [128, 128], "uint8"),
    "wq_in": ("sbuf", [128, 128], "float8_e4m3fn_x4"),
    "ws_in": ("sbuf", [128, 128], "uint8"),
    "xq": ("sbuf", [128, 256], "float8_e4m3fn_x4"),
    "xs": ("sbuf", [128, 256], "uint8"),
    "acc": ("psum", [128, 512], "float32"),
    "yt": ("sbuf", [128, 256], "float32"),
}
SEMAPHORES = ["w_in", "x_in", "wq_done", "xq_done", "arr_s", "arr_c", "sent", "mm", "cp", "out"]

RELAY_LAG = 3


def _bits(mask):
    return bin(mask).count("1")


def _plan(T, topo):
    cores, owner = list(T.cores), T.tables["OWNER"]

    def links(a, b):
        ca, cb = topo.chip(a), topo.chip(b)
        if ca == cb:
            return 0
        return 1 if (topo.mates(ca, cb) or topo.same_plane(ca, cb)) else 2

    trees, ports = [], set()
    for o in sorted(set(owner)):
        src = cores[o]
        users = [cores[r] for r in range(len(cores)) if owner[r] == o and r != o]
        relays = [d for d in users if topo.mates(topo.chip(src), topo.chip(d))]
        near = [d for d in users if links(src, d) < 2 and d not in relays]
        far = [d for d in users if links(src, d) == 2]
        for d in relays + near:
            if links(src, d):
                ports.add((topo.chip(d), topo.die(src)))
        trees.append((src, relays, near, far))

    sends = {}
    for src, relays, near, far in trees:
        given, direct = {f: [] for f in relays}, []
        for d in far:
            offers = []
            for f in relays:
                if links(f, d) < 2 and topo.may_write(f, d):
                    offers.append((RELAY_LAG + len(given[f]) + 1, f))
            if topo.may_write(src, d):
                offers.append((len(relays) + len(near) + len(direct) + 1, src))
            offers = [(t + (0.5 if (topo.chip(d), topo.die(s)) in ports else 0.0), s) for t, s in offers]
            first = min(t for t, s in offers)
            s = [s for t, s in offers if t == first][0]
            ports.add((topo.chip(d), topo.die(s)))
            (direct if s == src else given[s]).append(d)
        rest = direct + sorted(near, key=lambda d: -links(src, d))
        sends[src] = [grp for grp in (relays, rest) if grp]
        for f in relays:
            if given[f]:
                sends[f] = [given[f]]

    engines = {}
    for s in sends:
        for grp in sends[s]:
            for d in grp:
                engines[d] = _bits(_mask(topo, s, grp))
    return sends, engines


def _mask(topo, src, grp):
    m = topo.mask(src, grp[0])
    for d in grp[1:]:
        m &= topo.mask(src, d)
    return m


def rank_program(g, core, T, topo):
    rank = T.rank_of(core)
    if rank is None:
        return
    sem = T.sem
    owner = T.tables["OWNER"]
    holds = rank in owner
    own_w = owner[rank] == rank
    sends, engines = _plan(T, topo)

    if holds:
        g.sync.dma_start(T.wt[:], T.w[:]).then_inc(sem.w_in, 16)
    g.sync.dma_start(T.xt[:], T.x[:]).then_inc(sem.x_in, 16)

    if holds:
        g.vector.wait_ge(sem.w_in, 16)
        g.vector.quantize_mx(T.wq_own[:], T.ws_own[:], T.wt[:]).then_inc(sem.wq_done, 1)
    g.vector.wait_ge(sem.x_in, 16)
    g.vector.quantize_mx(T.xq[:], T.xs[:], T.xt[:]).then_inc(sem.xq_done, 1)

    left = 0
    if holds:
        g.wait_ge(sem.wq_done, 1)
    for grp in sends.get(core, []):
        mask = _mask(topo, core, grp)
        ids = [DstId(rid=topo.addr(d)[0], pnc=topo.addr(d)[1]) for d in grp]
        for piece in ("plane", "codes"):
            if piece == "plane":
                src = T.ws_own[:] if holds else T.ws_in[:]
                dst, arr = T.ws_in[:], sem.arr_s
            else:
                src = (T.wq_own[:] if holds else T.wq_in[:]).bitcast(dt.uint8)
                dst, arr = T.wq_in[:].bitcast(dt.uint8), sem.arr_c
            if not holds:
                g.wait_ge(arr, engines[core])
            g.remote_dma_fused(
                [RemoteDMATransfer(dst_ids=ids, dma_engine_mask=mask, remote_sem=arr,
                                   srcs=[src], dsts=[dst for d in grp])],
                local_sem=sem.sent)
            left += _bits(mask)
    if left:
        g.wait_ge(sem.sent, left)

    g.tensor.wait_ge(sem.xq_done, 1)
    if own_w:
        g.tensor.wait_ge(sem.wq_done, 1)
        wq, ws = T.wq_own, T.ws_own
    else:
        g.tensor.wait_ge(sem.arr_s, engines[core])
        g.tensor.wait_ge(sem.arr_c, engines[core])
        wq, ws = T.wq_in, T.ws_in
    g.tensor.matmul_mx(T.acc[:, 0:256], wq[:], ws[:], T.xq[:], T.xs[:], True, True).then_inc(sem.mm, 1)
    g.vector.wait_ge(sem.mm, 1)
    g.vector.tensor_copy(T.yt[:], T.acc[:, 0:256]).then_inc(sem.cp, 1)
    g.sync.wait_ge(sem.cp, 1)
    g.sync.dma_start(T.y[:], T.yt[:]).then_inc(sem.out, 16)
    g.sync.wait_ge(sem.out, 16)
